import numpy as np
import ml_dtypes


def mxq(x, axis, fmt="e4m3"):
    dtype, down = {"e4m3": (ml_dtypes.float8_e4m3fn, 7), "e5m2": (ml_dtypes.float8_e5m2, 14)}[fmt]
    v = np.moveaxis(np.asarray(x, np.float32).astype(ml_dtypes.bfloat16).astype(np.float64), axis, -1)
    blocks = v.reshape(v.shape[:-1] + (-1, 32))
    amax = np.abs(blocks).max(-1, keepdims=True)
    byte = np.maximum(np.where(amax > 0, np.frexp(amax)[1] - 1 + 127, 0) - down, 1)
    scale = np.exp2(byte - 127.0)
    codes = (blocks / scale).astype(np.float32).astype(dtype).astype(np.float64)
    return np.moveaxis((codes * scale).reshape(v.shape), -1, axis)


WIDE = False


def mx_kscale(k):
    if not WIDE:
        return np.ones(k)
    levels = np.array([10, -10, 5, -5, 0])
    if k % 512:
        return np.exp2(np.random.permutation(np.resize(levels, k // 32))).repeat(32)
    a = np.empty((k // 512, 16))
    for p in range(k // 512):
        a[p, :8] = np.random.permutation(np.resize(levels, 8))
        for g in range(8):
            far = levels[np.abs(levels - a[p, g]) >= 10]
            a[p, g + 8] = far[np.random.randint(len(far))]
    return np.exp2(a.ravel()).repeat(32)


def f64(x):
    return np.asarray(x).astype(np.float64)


def striped(idx):
    return np.tile(idx.reshape(-1, 16).T, (8, 1)).astype(np.uint16)


def unstriped(offs):
    return offs[:16].T.reshape(-1).astype(np.int64)


E2M1 = np.array([0.0, 0.5, 1.0, 1.5, 2.0, 3.0, 4.0, 6.0, -0.0, -0.5, -1.0, -1.5, -2.0, -3.0, -4.0, -6.0])


def pack_weight(w, fmt):
    k, n = w.shape
    w = f64(np.asarray(w, np.float32).astype(ml_dtypes.bfloat16)).reshape(k // 32, 32, n)
    amax = np.abs(w).max(1)
    if fmt == "e4m3":
        byte = np.frexp(amax)[1] - 1 + 127 - 7
    else:
        mant, ex = np.frexp(amax / 6.0)
        byte = np.where(mant > 0.5, ex, ex - 1) + 127
    byte = np.clip(np.where(amax > 0, byte, 1), 1, 254)
    scaled = (w * np.exp2(127.0 - byte)[:, None, :]).reshape(k, n).astype(np.float32)
    by_word = np.ascontiguousarray(scaled.reshape(k // 512, 128, 4, n).transpose(0, 1, 3, 2))
    if fmt == "e4m3":
        words = by_word.astype(ml_dtypes.float8_e4m3fn).view(np.uint8)
    else:
        c = by_word.astype(ml_dtypes.float4_e2m1fn).view(np.uint8) & 0xF
        words = (c[..., 0::2] | (c[..., 1::2] << 4)).reshape(k // 512, 128, 2 * n)
    return np.ascontiguousarray(words), np.ascontiguousarray(byte.astype(np.uint8).reshape(k // 512, 16, n))


def unpack_weight(words, scales, fmt):
    g, _, n = scales.shape
    words = np.ascontiguousarray(words).reshape(g, 128, n, -1)
    if fmt == "e4m3":
        vals = words.view(ml_dtypes.float8_e4m3fn).astype(np.float64)
    else:
        nib = np.empty((g, 128, n, 4), np.uint8)
        nib[..., 0::2] = words & 0xF
        nib[..., 1::2] = words >> 4
        vals = E2M1[nib]
    vals = vals * np.repeat(np.exp2(scales.astype(np.float64) - 127.0), 8, axis=1)[..., None]
    return vals.transpose(0, 1, 3, 2).reshape(g * 512, n)


K, T, E, C, N = 2560, 768, 12, 128, 128
K8 = 1024


def by_expert(wq, xq):
    return np.concatenate([wq[e].T @ xq[:, e * C:(e + 1) * C] for e in range(E)], axis=1)


def setup_inputs():
    n = np.random.standard_normal
    s = mx_kscale(K)[:, None]
    first = np.random.permutation(np.repeat(np.arange(E), T // E))
    second = (first + 1 + np.random.permutation(np.repeat(np.arange(E - 1), -(-T // (E - 1)))[:T])) % E
    while np.bincount(second, minlength=E).max() != T // E:
        load = np.bincount(second, minlength=E); hi, lo = int(load.argmax()), int(load.argmin())
        t = np.flatnonzero((second == hi) & (first != lo))[0]; second[t] = lo
    slot_token = np.empty(E * C, np.int64); pos = np.empty((2, T), np.int64); fill = np.zeros(E, np.int64)
    place = np.stack([np.random.permutation(C) for _ in range(E)])
    for r, deal in enumerate((first, second)):
        for t in np.random.permutation(T):
            e = deal[t]; j = e * C + place[e, fill[e]]; fill[e] += 1; slot_token[j] = t; pos[r, t] = j
    g = np.random.uniform(0.2, 0.8, T)
    w = n((E, K, N)) / np.sqrt(K) / s[None]
    w8 = [pack_weight(m[:K8], "e4m3") for m in w]
    w4 = [pack_weight(m[K8:], "e2m1") for m in w]
    return {
        "xT": (n((K, T)) * s).astype(np.float32),
        "w8_words": np.stack([m[0] for m in w8]),
        "w8_scales": np.stack([m[1] for m in w8]),
        "w4_words": np.stack([m[0] for m in w4]),
        "w4_scales": np.stack([m[1] for m in w4]),
        "gate": np.stack([np.tile(g, (N, 1)), np.tile(1.0 - g, (N, 1))]).astype(np.float32),
        "offs": striped(slot_token),
        "pos1": striped(pos[0]),
        "pos2": striped(pos[1]),
    }


def reference(xT, w8_words, w8_scales, w4_words, w4_scales, gate, offs, pos1, pos2):
    idx = unstriped(offs)
    w = np.stack([np.concatenate([unpack_weight(w8_words[e], w8_scales[e], "e4m3"), unpack_weight(w4_words[e], w4_scales[e], "e2m1")]) for e in range(E)])
    xq = mxq(f64(xT)[:, idx], 0, "e4m3")
    y = by_expert(w, xq)
    return f64(gate[0]) * y[:, unstriped(pos1)] + f64(gate[1]) * y[:, unstriped(pos2)]

@@ -1,0 +1,197 @@
+from contextlib import ExitStack
+
+import concourse.mybir as mybir
+
+F32 = mybir.dt.float32
+BF16 = mybir.dt.bfloat16
+I32 = mybir.dt.int32
+U32 = mybir.dt.uint32
+U16 = mybir.dt.uint16
+U8 = mybir.dt.uint8
+FP8X4 = mybir.dt.float8_e4m3fn_x4
+FP4X4 = mybir.dt.float4_e2m1fn_x4
+COPY = mybir.ActivationFunctionType.Copy
+MULT = mybir.AluOpType.mult
+ADD = mybir.AluOpType.add
+
+P = 128
+K, T, E, C, N = 2560, 768, 12, 128, 128
+S = E * C
+PASSES = K // 512
+FLOPS = 2 * K * N * S
+
+CHUNKS = ((0, 512), (512, 768))
+WIDE = 2048
+ORDER = (2, 0, 1, 3, 4)
+ROW = {2: 0, 3: 0, 0: 4, 1: 8, 4: 12}
+SPLIT_LOADS = 3
+
+
+def tile_moe_pln_lin_none_kernel(tc, xT, w8_words, w8_scales, w4_words, w4_scales, gate, offs, pos1, pos2, out):
+    nc = tc.nc
+    with ExitStack() as ctx:
+        keep = ctx.enter_context(tc.tile_pool(name="keep", bufs=1))
+        psum = ctx.enter_context(tc.psum_pool(name="psum", bufs=1))
+
+        offs_t = keep.tile([P, S // 16], U16, name="offs_t")
+        pos1_t = keep.tile([P, T // 16], U16, name="pos1_t")
+        pos2_t = keep.tile([P, T // 16], U16, name="pos2_t")
+        gate_t = keep.tile([P, 2, T], F32, name="gate_t")
+
+        plane_a = keep.tile([P, WIDE], U8, name="plane_a", align_bytes=64)
+        plane_b = keep.tile([P, WIDE], U8, name="plane_b", align_bytes=64)
+        w8s = keep.tile([P, E, 2, N], U8, name="w8s", align_bytes=64)
+        w4s = keep.tile([P, E, 3, N], U8, name="w4s", align_bytes=64)
+        moved = keep.tile([P, S], U8, name="moved", align_bytes=64)
+        for t in (plane_b[:], plane_a[:], w8s[:].rearrange("p e a n -> p (e a n)"), w4s[:].rearrange("p e a n -> p (e a n)"), moved[:]):
+            nc.gpsimd.memset(t.bitcast(I32), 0)
+        codes = {}
+        for a in ORDER:
+            wide = a in ORDER[:3]
+            codes[a] = keep.tile([P, WIDE if wide else T], I32, name=f"codes{a}", align_bytes=64)
+            if wide:
+                nc.vector.memset(codes[a][:, T:WIDE], 0)
+
+        x_view = xT.rearrange("(a p j) t -> a p j t", p=P, j=4)
+        raw = {}
+        for i, a in enumerate(ORDER):
+            raw[a] = keep.tile([P, 4, T], F32, name=f"raw{a}")
+            for lo, hi in CHUNKS if i < SPLIT_LOADS else ((0, T),):
+                nc.sync.dma_start(raw[a][:, :, lo:hi], x_view[a][:, :, lo:hi])
+            if i == 0:
+                nc.sync.dma_start(offs_t[:], offs)
+        for q in range(4):
+            nc.sync.dma_start(
+                w4s[32 * q : 32 * q + 4].rearrange("p e a n -> p (e a) n").bitcast(I32),
+                w4_scales[:, :, 4 * q : 4 * q + 4, :].rearrange("e a q n -> q (e a) n").bitcast(I32),
+            )
+        for q in range(4):
+            nc.sync.dma_start(
+                w8s[32 * q : 32 * q + 4].rearrange("p e a n -> p (e a) n").bitcast(I32),
+                w8_scales[:, :, 4 * q : 4 * q + 4, :].rearrange("e a q n -> q (e a) n").bitcast(I32),
+            )
+        w8_view = w8_words.rearrange("e a p n r -> a p e (n r)")
+        w4_view = w4_words.rearrange("e a p b -> a p e b")
+        wt = {}
+        for a in ORDER:
+            if a < 2:
+                wt[a] = keep.tile([P, E, 4 * N], U8, name=f"w{a}", align_bytes=64)
+                nc.sync.dma_start(wt[a][:].bitcast(I32), w8_view[a].bitcast(I32))
+            else:
+                wt[a] = keep.tile([P, E, 2 * N], U8, name=f"w{a}", align_bytes=64)
+                nc.sync.dma_start(wt[a][:].bitcast(I32), w4_view[a - 2].bitcast(I32))
+        nc.sync.dma_start(pos1_t[:], pos1)
+        nc.sync.dma_start(pos2_t[:], pos2)
+        nc.sync.dma_start(gate_t[:], gate.rearrange("g p t -> p g t"))
+
+        grouped = [keep.tile([P, T, 4], BF16, name=f"grouped{a}", align_bytes=64) for a in range(PASSES)]
+        slot_words = [keep.tile([P, S], U32, name=f"slot_words{a}", align_bytes=64) for a in range(PASSES)]
+        bytes_a = keep.tile([P, S], U8, name="bytes_a", align_bytes=64)
+        bytes_b = keep.tile([P, S], U8, name="bytes_b", align_bytes=64)
+        y = keep.tile([P, S], F32, name="y")
+
+        def cast(a, lo, hi, on_vector=False):
+            dst = grouped[a][:, lo:hi, :].rearrange("p (c i) t -> p c t i", i=4)
+            src = raw[a][:, :, lo:hi].rearrange("p t (c i) -> p c t i", i=4)
+            if on_vector:
+                nc.vector.tensor_copy(dst, src)
+            else:
+                nc.scalar.activation(dst, src, COPY)
+
+        def quantise(a):
+            plane = plane_b if a == ORDER[0] else plane_a
+            for lo, hi in CHUNKS:
+                nc.vector.quantize_mx(
+                    out=codes[a][:, lo:hi].bitcast(FP8X4),
+                    scales=plane[ROW[a] : P, lo:hi],
+                    in_=grouped[a][:, lo:hi, :].rearrange("p t j -> p (t j)"),
+                )
+
+        def gather_words(a, lo=0, hi=S):
+            nc.vector.tensor_copy(slot_words[a][:, lo:hi], codes[a][:].bitcast(U32).indirect(offs_t[:, lo // 16 : hi // 16]))
+
+        def gather_bytes(dst, plane):
+            nc.vector.tensor_copy(dst[:], plane[:].indirect(offs_t[:]))
+
+        banks = {}
+
+        def multiply(a, e):
+            if a == ORDER[0]:
+                banks[e] = psum.tile([N, C], F32, name=f"bank{e % 8}")
+            cols = slice(e * C, (e + 1) * C)
+            if a < 2:
+                lhsT, lscale = wt[a][:, e, :].bitcast(FP8X4), w8s[:, e, a, :]
+            else:
+                lhsT, lscale = wt[a][:, e, :].bitcast(FP4X4), w4s[:, e, a - 2, :]
+            if a == ORDER[0]:
+                rscale = bytes_b[:, cols]
+            elif a == 4:
+                rscale = moved[:, cols]
+            else:
+                rscale = bytes_a[ROW[a] : P, cols]
+            nc.tensor.matmul_mx(
+                out=banks[e][:], lhsT=lhsT, lhsT_scale=lscale,
+                rhs=slot_words[a][:, cols].bitcast(FP8X4), rhs_scale=rscale,
+                start=(a == ORDER[0]), stop=(a == ORDER[-1]),
+            )
+
+        def empty(e, on_vector):
+            dst = y[:, e * C : (e + 1) * C]
+            if on_vector:
+                nc.vector.tensor_copy(dst, banks[e][:])
+            else:
+                nc.scalar.copy(dst, banks[e][:])
+
+        cast(2, 0, 320, on_vector=True)
+        cast(2, 320, 512)
+        cast(2, 512, 704, on_vector=True)
+        cast(2, 704, 768)
+        quantise(2)
+        for a in (0, 1, 3, 4):
+            for lo, hi in CHUNKS:
+                cast(a, lo, hi)
+        gather_words(2)
+        gather_bytes(bytes_b, plane_b)
+        for e in range(8):
+            multiply(2, e)
+        quantise(0)
+        gather_words(0)
+        quantise(1)
+        gather_words(1)
+        quantise(3)
+        quantise(4)
+        gather_bytes(bytes_a, plane_a)
+        for r in range(4):
+            nc.scalar.dma_start(moved[r:P:32, :].bitcast(I32), bytes_a[12 + r : P : 32, :].bitcast(I32))
+        for a in (0, 1):
+            for e in range(8):
+                multiply(a, e)
+        for lo, hi in ((0, 512), (512, 1024), (1024, 1280), (1280, 1536)):
+            gather_words(3, lo, hi)
+            gather_words(4, lo, hi)
+            experts = range(lo // C, hi // C)
+            for a in (3, 4):
+                for e in experts:
+                    multiply(a, e)
+            for e in experts:
+                empty(e, on_vector=(e in (9, 11)))
+            if lo == 0:
+                for a in (2, 0, 1):
+                    for e in range(8, 12):
+                        multiply(a, e)
+
+        halves = ((0, 384), (384, 768))
+        part = {}
+
+        def finish(lo, hi):
+            total = keep.tile([P, hi - lo], F32, name=f"total{lo}")
+            nc.vector.tensor_tensor(total[:], part[lo, 0][:], part[lo, 1][:], ADD)
+            nc.sync.dma_start(out[:, lo:hi], total[:])
+
+        for lo, hi in halves:
+            for g, pos in enumerate((pos1_t, pos2_t)):
+                part[lo, g] = keep.tile([P, hi - lo], F32, name=f"part{lo}_{g}")
+                nc.vector.tensor_tensor(part[lo, g][:], y[:].indirect(pos[:, lo // 16 : hi // 16]), gate_t[:, g, lo:hi], MULT)
+                if lo and g == 0:
+                    finish(0, 384)
+        finish(384, 768)

@@ -20,11 +20,12 @@ S = E * C
 PASSES = K // 512
 FLOPS = 2 * K * N * S
 
-CHUNKS = ((0, 512), (512, 768))
+ORDER = (2, 3, 0, 1, 4)
+ROW = {2: 0, 3: 4, 4: 0, 0: 4, 1: 8}
 WIDE = 2048
-ORDER = (2, 0, 1, 3, 4)
-ROW = {2: 0, 3: 0, 0: 4, 1: 8, 4: 12}
-SPLIT_LOADS = 3
+PIECES = ((0, 512), (512, 768))
+LOADS = {2: ((0, 512), (512, 768)), 3: ((0, 256), (256, 512), (512, 768))}
+GROUP = 4 * (2 * 4 * N + 3 * 2 * N)
 
 
 def tile_moe_pln_lin_none_kernel(tc, xT, w8_words, w8_scales, w4_words, w4_scales, gate, offs, pos1, pos2, out):
@@ -38,12 +39,12 @@ def tile_moe_pln_lin_none_kernel(tc, xT, w8_words, w8_scales, w4_words, w4_scale
         pos2_t = keep.tile([P, T // 16], U16, name="pos2_t")
         gate_t = keep.tile([P, 2, T], F32, name="gate_t")
 
-        plane_a = keep.tile([P, WIDE], U8, name="plane_a", align_bytes=64)
-        plane_b = keep.tile([P, WIDE], U8, name="plane_b", align_bytes=64)
+        plane_a = keep.tile([P, WIDE], U8, name="plane_a", tag="shared_a", align_bytes=64)
+        plane_b = keep.tile([P, WIDE], U8, name="plane_b", tag="shared", align_bytes=64)
         w8s = keep.tile([P, E, 2, N], U8, name="w8s", align_bytes=64)
         w4s = keep.tile([P, E, 3, N], U8, name="w4s", align_bytes=64)
         moved = keep.tile([P, S], U8, name="moved", align_bytes=64)
-        for t in (plane_b[:], plane_a[:], w8s[:].rearrange("p e a n -> p (e a n)"), w4s[:].rearrange("p e a n -> p (e a n)"), moved[:]):
+        for t in (plane_b[:], w8s[:].rearrange("p e a n -> p (e a n)"), w4s[:].rearrange("p e a n -> p (e a n)"), plane_a[:], moved[:]):
             nc.gpsimd.memset(t.bitcast(I32), 0)
         codes = {}
         for a in ORDER:
@@ -55,57 +56,53 @@ def tile_moe_pln_lin_none_kernel(tc, xT, w8_words, w8_scales, w4_words, w4_scale
         x_view = xT.rearrange("(a p j) t -> a p j t", p=P, j=4)
         raw = {}
         for i, a in enumerate(ORDER):
-            raw[a] = keep.tile([P, 4, T], F32, name=f"raw{a}")
-            for lo, hi in CHUNKS if i < SPLIT_LOADS else ((0, T),):
-                nc.sync.dma_start(raw[a][:, :, lo:hi], x_view[a][:, :, lo:hi])
+            for lo, hi in LOADS.get(a, ((0, T),)):
+                part = keep.tile([P, 4, hi - lo], F32, name=f"raw{a}_{lo}")
+                nc.sync.dma_start(part[:], x_view[a][:, :, lo:hi])
+                raw.setdefault(a, []).append((lo, hi, part))
             if i == 0:
                 nc.sync.dma_start(offs_t[:], offs)
-        for q in range(4):
-            nc.sync.dma_start(
-                w4s[32 * q : 32 * q + 4].rearrange("p e a n -> p (e a) n").bitcast(I32),
-                w4_scales[:, :, 4 * q : 4 * q + 4, :].rearrange("e a q n -> q (e a) n").bitcast(I32),
-            )
-        for q in range(4):
-            nc.sync.dma_start(
-                w8s[32 * q : 32 * q + 4].rearrange("p e a n -> p (e a) n").bitcast(I32),
-                w8_scales[:, :, 4 * q : 4 * q + 4, :].rearrange("e a q n -> q (e a) n").bitcast(I32),
-            )
-        w8_view = w8_words.rearrange("e a p n r -> a p e (n r)")
-        w4_view = w4_words.rearrange("e a p b -> a p e b")
-        wt = {}
-        for a in ORDER:
-            if a < 2:
-                wt[a] = keep.tile([P, E, 4 * N], U8, name=f"w{a}", align_bytes=64)
-                nc.sync.dma_start(wt[a][:].bitcast(I32), w8_view[a].bitcast(I32))
-            else:
-                wt[a] = keep.tile([P, E, 2 * N], U8, name=f"w{a}", align_bytes=64)
-                nc.sync.dma_start(wt[a][:].bitcast(I32), w4_view[a - 2].bitcast(I32))
-        nc.sync.dma_start(pos1_t[:], pos1)
-        nc.sync.dma_start(pos2_t[:], pos2)
-        nc.sync.dma_start(gate_t[:], gate.rearrange("g p t -> p g t"))
+        for scales, source in ((w4s, w4_scales), (w8s, w8_scales)):
+            for q in range(4):
+                nc.sync.dma_start(
+                    scales[32 * q : 32 * q + 4].rearrange("p e a n -> p (e a) n").bitcast(I32),
+                    source[:, :, 4 * q : 4 * q + 4, :].rearrange("e a q n -> q (e a) n").bitcast(I32),
+                )
+        w8_view = w8_words.rearrange("e a p n r -> p (e a) (n r)")
+        w4_view = w4_words.rearrange("e a p b -> p (e a) b")
+
+        def load_words(dst, g):
+            half = 4 * 2 * 4 * N
+            nc.sync.dma_start(dst[:, :half].rearrange("p (x b) -> p x b", b=4 * N).bitcast(I32), w8_view[:, 8 * g : 8 * g + 8, :].bitcast(I32))
+            nc.sync.dma_start(dst[:, half:].rearrange("p (x b) -> p x b", b=2 * N).bitcast(I32), w4_view[:, 12 * g : 12 * g + 12, :].bitcast(I32))
+
+        words_0 = keep.tile([P, GROUP], U8, name="words_0", align_bytes=64)
+        load_words(words_0[:], 0)
+        words = [words_0[:]]
 
         grouped = [keep.tile([P, T, 4], BF16, name=f"grouped{a}", align_bytes=64) for a in range(PASSES)]
-        slot_words = [keep.tile([P, S], U32, name=f"slot_words{a}", align_bytes=64) for a in range(PASSES)]
+        slot_words = {a: keep.tile([P, S], U32, name=f"slot_words{a}", align_bytes=64) for a in (2, 3, 0, 4)}
         bytes_a = keep.tile([P, S], U8, name="bytes_a", align_bytes=64)
         bytes_b = keep.tile([P, S], U8, name="bytes_b", align_bytes=64)
         y = keep.tile([P, S], F32, name="y")
 
         def cast(a, lo, hi, on_vector=False):
-            dst = grouped[a][:, lo:hi, :].rearrange("p (c i) t -> p c t i", i=4)
-            src = raw[a][:, :, lo:hi].rearrange("p t (c i) -> p c t i", i=4)
-            if on_vector:
-                nc.vector.tensor_copy(dst, src)
-            else:
-                nc.scalar.activation(dst, src, COPY)
+            for base, end, part in raw[a]:
+                if base <= lo and hi <= end:
+                    dst = grouped[a][:, lo:hi, :].rearrange("p (c i) t -> p c t i", i=4)
+                    from_raw = part[:, :, lo - base : hi - base].rearrange("p t (c i) -> p c t i", i=4)
+                    if on_vector:
+                        nc.vector.tensor_copy(dst, from_raw)
+                    else:
+                        nc.scalar.activation(dst, from_raw, COPY)
 
-        def quantise(a):
-            plane = plane_b if a == ORDER[0] else plane_a
-            for lo, hi in CHUNKS:
-                nc.vector.quantize_mx(
-                    out=codes[a][:, lo:hi].bitcast(FP8X4),
-                    scales=plane[ROW[a] : P, lo:hi],
-                    in_=grouped[a][:, lo:hi, :].rearrange("p t j -> p (t j)"),
-                )
+        def quantise(a, lo, hi):
+            plane = plane_b if a in ORDER[:2] else plane_a
+            nc.vector.quantize_mx(
+                out=codes[a][:, lo:hi].bitcast(FP8X4),
+                scales=plane[ROW[a] : P, lo:hi],
+                in_=grouped[a][:, lo:hi, :].rearrange("p t j -> p (t j)"),
+            )
 
         def gather_words(a, lo=0, hi=S):
             nc.vector.tensor_copy(slot_words[a][:, lo:hi], codes[a][:].bitcast(U32).indirect(offs_t[:, lo // 16 : hi // 16]))
@@ -115,27 +112,30 @@ def tile_moe_pln_lin_none_kernel(tc, xT, w8_words, w8_scales, w4_words, w4_scale
 
         banks = {}
 
-        def multiply(a, e):
-            if a == ORDER[0]:
-                banks[e] = psum.tile([N, C], F32, name=f"bank{e % 8}")
-            cols = slice(e * C, (e + 1) * C)
-            if a < 2:
-                lhsT, lscale = wt[a][:, e, :].bitcast(FP8X4), w8s[:, e, a, :]
-            else:
-                lhsT, lscale = wt[a][:, e, :].bitcast(FP4X4), w4s[:, e, a - 2, :]
-            if a == ORDER[0]:
-                rscale = bytes_b[:, cols]
-            elif a == 4:
-                rscale = moved[:, cols]
-            else:
-                rscale = bytes_a[ROW[a] : P, cols]
-            nc.tensor.matmul_mx(
-                out=banks[e][:], lhsT=lhsT, lhsT_scale=lscale,
-                rhs=slot_words[a][:, cols].bitcast(FP8X4), rhs_scale=rscale,
-                start=(a == ORDER[0]), stop=(a == ORDER[-1]),
-            )
+        def multiply(a, experts):
+            for e in experts:
+                if a == ORDER[0]:
+                    banks[e] = psum.tile([N, C], F32, name=f"bank{e % 8}")
+                cols = slice(e * C, (e + 1) * C)
+                if a < 2:
+                    start = ((e % 4) * 2 + a) * 4 * N
+                    lhsT, lscale = words[e // 4][:, start : start + 4 * N].bitcast(FP8X4), w8s[:, e, a, :]
+                else:
+                    start = 4 * 2 * 4 * N + ((e % 4) * 3 + a - 2) * 2 * N
+                    lhsT, lscale = words[e // 4][:, start : start + 2 * N].bitcast(FP4X4), w4s[:, e, a - 2, :]
+                if a == 2:
+                    rscale = bytes_b[:, cols]
+                elif a == 3:
+                    rscale = moved[:, cols]
+                else:
+                    rscale = bytes_a[ROW[a] : P, cols]
+                nc.tensor.matmul_mx(
+                    out=banks[e][:], lhsT=lhsT, lhsT_scale=lscale,
+                    rhs=slot_words[a][:, cols].bitcast(FP8X4), rhs_scale=rscale,
+                    start=(a == ORDER[0]), stop=(a == ORDER[-1]),
+                )
 
-        def empty(e, on_vector):
+        def empty(e, on_vector=False):
             dst = y[:, e * C : (e + 1) * C]
             if on_vector:
                 nc.vector.tensor_copy(dst, banks[e][:])
@@ -144,43 +144,62 @@ def tile_moe_pln_lin_none_kernel(tc, xT, w8_words, w8_scales, w4_words, w4_scale
 
         cast(2, 0, 320, on_vector=True)
         cast(2, 320, 512)
-        cast(2, 512, 704, on_vector=True)
-        cast(2, 704, 768)
-        quantise(2)
-        for a in (0, 1, 3, 4):
-            for lo, hi in CHUNKS:
+        quantise(2, 0, 512)
+        cast(2, 512, 640, on_vector=True)
+        cast(2, 640, 768)
+        quantise(2, 512, 768)
+        for lo in (0, 256, 512):
+            cast(3, lo, lo + 256)
+        for a in (0, 1, 4):
+            for lo, hi in PIECES:
                 cast(a, lo, hi)
         gather_words(2)
+        for lo, hi in PIECES:
+            quantise(3, lo, hi)
+        gather_words(3)
         gather_bytes(bytes_b, plane_b)
-        for e in range(8):
-            multiply(2, e)
-        quantise(0)
-        gather_words(0)
-        quantise(1)
-        gather_words(1)
-        quantise(3)
-        quantise(4)
-        gather_bytes(bytes_a, plane_a)
         for r in range(4):
-            nc.scalar.dma_start(moved[r:P:32, :].bitcast(I32), bytes_a[12 + r : P : 32, :].bitcast(I32))
-        for a in (0, 1):
-            for e in range(8):
-                multiply(a, e)
-        for lo, hi in ((0, 512), (512, 1024), (1024, 1280), (1280, 1536)):
-            gather_words(3, lo, hi)
-            gather_words(4, lo, hi)
-            experts = range(lo // C, hi // C)
-            for a in (3, 4):
-                for e in experts:
-                    multiply(a, e)
+            nc.sync.dma_start(moved[r:P:32, :].bitcast(I32), bytes_b[4 + r : P : 32, :].bitcast(I32))
+        later = keep.tile([P, 2 * GROUP], U8, name="later", tag="shared", align_bytes=64)
+        for g in (1, 2):
+            words.append(later[:, (g - 1) * GROUP : g * GROUP])
+            load_words(words[g], g)
+        nc.sync.dma_start(pos1_t[:], pos1)
+        nc.sync.dma_start(pos2_t[:], pos2)
+        nc.sync.dma_start(gate_t[:], gate.rearrange("g p t -> p g t"))
+        A, B, CD = range(0, 4), range(4, 8), range(8, 12)
+        for experts in (A, B):
+            for a in (2, 3):
+                multiply(a, experts)
+        for lo, hi in PIECES:
+            quantise(0, lo, hi)
+        gather_words(0, 0, 1024)
+        for lo, hi in PIECES:
+            quantise(1, lo, hi)
+        gather_words(0, 1024, S)
+        for lo, hi in PIECES:
+            quantise(4, lo, hi)
+        gather_bytes(bytes_a, plane_a)
+        slot_words[1] = keep.tile([P, S], U32, name="slot_words1", tag="shared_a", align_bytes=64)
+        multiply(0, A)
+        multiply(0, B)
+        for lo, experts in ((0, A), (512, B)):
+            gather_words(1, lo, lo + 512)
+            gather_words(4, lo, lo + 512)
+            multiply(1, experts)
+            multiply(4, experts)
             for e in experts:
-                empty(e, on_vector=(e in (9, 11)))
-            if lo == 0:
-                for a in (2, 0, 1):
-                    for e in range(8, 12):
-                        multiply(a, e)
+                empty(e)
+        gather_words(1, 1024, S)
+        for a in (2, 3, 0, 1):
+            multiply(a, CD)
+        for lo in (1024, 1280):
+            gather_words(4, lo, lo + 256)
+            e = lo // C
+            multiply(4, (e, e + 1))
+            empty(e)
+            empty(e + 1, on_vector=True)
 
-        halves = ((0, 384), (384, 768))
         part = {}
 
         def finish(lo, hi):
@@ -188,7 +207,7 @@ def tile_moe_pln_lin_none_kernel(tc, xT, w8_words, w8_scales, w4_words, w4_scale
             nc.vector.tensor_tensor(total[:], part[lo, 0][:], part[lo, 1][:], ADD)
             nc.sync.dma_start(out[:, lo:hi], total[:])
 
-        for lo, hi in halves:
+        for lo, hi in ((0, 384), (384, 768)):
             for g, pos in enumerate((pos1_t, pos2_t)):
                 part[lo, g] = keep.tile([P, hi - lo], F32, name=f"part{lo}_{g}")
                 nc.vector.tensor_tensor(part[lo, g][:], y[:].indirect(pos[:, lo // 16 : hi // 16]), gate_t[:, g, lo:hi], MULT)

from contextlib import ExitStack

import concourse.mybir as mybir

F32 = mybir.dt.float32
BF16 = mybir.dt.bfloat16
I32 = mybir.dt.int32
U32 = mybir.dt.uint32
U16 = mybir.dt.uint16
U8 = mybir.dt.uint8
FP8X4 = mybir.dt.float8_e4m3fn_x4
FP4X4 = mybir.dt.float4_e2m1fn_x4
COPY = mybir.ActivationFunctionType.Copy
MULT = mybir.AluOpType.mult
ADD = mybir.AluOpType.add

P = 128
K, T, E, C, N = 2560, 768, 12, 128, 128
S = E * C
PASSES = K // 512
FLOPS = 2 * K * N * S

ORDER = (2, 3, 0, 1, 4)
ROW = {2: 0, 3: 4, 4: 0, 0: 4, 1: 8}
WIDE = 2048
PIECES = ((0, 512), (512, 768))
LOADS = {2: ((0, 512), (512, 768)), 3: ((0, 256), (256, 512), (512, 768))}
GROUP = 4 * (2 * 4 * N + 3 * 2 * N)


def tile_moe_pln_lin_none_kernel(tc, xT, w8_words, w8_scales, w4_words, w4_scales, gate, offs, pos1, pos2, out):
    nc = tc.nc
    with ExitStack() as ctx:
        keep = ctx.enter_context(tc.tile_pool(name="keep", bufs=1))
        psum = ctx.enter_context(tc.psum_pool(name="psum", bufs=1))

        offs_t = keep.tile([P, S // 16], U16, name="offs_t")
        pos1_t = keep.tile([P, T // 16], U16, name="pos1_t")
        pos2_t = keep.tile([P, T // 16], U16, name="pos2_t")
        gate_t = keep.tile([P, 2, T], F32, name="gate_t")

        plane_a = keep.tile([P, WIDE], U8, name="plane_a", tag="shared_a", align_bytes=64)
        plane_b = keep.tile([P, WIDE], U8, name="plane_b", tag="shared", align_bytes=64)
        w8s = keep.tile([P, E, 2, N], U8, name="w8s", align_bytes=64)
        w4s = keep.tile([P, E, 3, N], U8, name="w4s", align_bytes=64)
        moved = keep.tile([P, S], U8, name="moved", align_bytes=64)
        for t in (plane_b[:], w8s[:].rearrange("p e a n -> p (e a n)"), w4s[:].rearrange("p e a n -> p (e a n)"), plane_a[:], moved[:]):
            nc.gpsimd.memset(t.bitcast(I32), 0)
        codes = {}
        for a in ORDER:
            wide = a in ORDER[:3]
            codes[a] = keep.tile([P, WIDE if wide else T], I32, name=f"codes{a}", align_bytes=64)
            if wide:
                nc.vector.memset(codes[a][:, T:WIDE], 0)

        x_view = xT.rearrange("(a p j) t -> a p j t", p=P, j=4)
        raw = {}
        for i, a in enumerate(ORDER):
            for lo, hi in LOADS.get(a, ((0, T),)):
                part = keep.tile([P, 4, hi - lo], F32, name=f"raw{a}_{lo}")
                nc.sync.dma_start(part[:], x_view[a][:, :, lo:hi])
                raw.setdefault(a, []).append((lo, hi, part))
            if i == 0:
                nc.sync.dma_start(offs_t[:], offs)
        for scales, source in ((w4s, w4_scales), (w8s, w8_scales)):
            for q in range(4):
                nc.sync.dma_start(
                    scales[32 * q : 32 * q + 4].rearrange("p e a n -> p (e a) n").bitcast(I32),
                    source[:, :, 4 * q : 4 * q + 4, :].rearrange("e a q n -> q (e a) n").bitcast(I32),
                )
        w8_view = w8_words.rearrange("e a p n r -> p (e a) (n r)")
        w4_view = w4_words.rearrange("e a p b -> p (e a) b")

        def load_words(dst, g):
            half = 4 * 2 * 4 * N
            nc.sync.dma_start(dst[:, :half].rearrange("p (x b) -> p x b", b=4 * N).bitcast(I32), w8_view[:, 8 * g : 8 * g + 8, :].bitcast(I32))
            nc.sync.dma_start(dst[:, half:].rearrange("p (x b) -> p x b", b=2 * N).bitcast(I32), w4_view[:, 12 * g : 12 * g + 12, :].bitcast(I32))

        words_0 = keep.tile([P, GROUP], U8, name="words_0", align_bytes=64)
        load_words(words_0[:], 0)
        words = [words_0[:]]

        grouped = [keep.tile([P, T, 4], BF16, name=f"grouped{a}", align_bytes=64) for a in range(PASSES)]
        slot_words = {a: keep.tile([P, S], U32, name=f"slot_words{a}", align_bytes=64) for a in (2, 3, 0, 4)}
        bytes_a = keep.tile([P, S], U8, name="bytes_a", align_bytes=64)
        bytes_b = keep.tile([P, S], U8, name="bytes_b", align_bytes=64)
        y = keep.tile([P, S], F32, name="y")

        def cast(a, lo, hi, on_vector=False):
            for base, end, part in raw[a]:
                if base <= lo and hi <= end:
                    dst = grouped[a][:, lo:hi, :].rearrange("p (c i) t -> p c t i", i=4)
                    from_raw = part[:, :, lo - base : hi - base].rearrange("p t (c i) -> p c t i", i=4)
                    if on_vector:
                        nc.vector.tensor_copy(dst, from_raw)
                    else:
                        nc.scalar.activation(dst, from_raw, COPY)

        def quantise(a, lo, hi):
            plane = plane_b if a in ORDER[:2] else plane_a
            nc.vector.quantize_mx(
                out=codes[a][:, lo:hi].bitcast(FP8X4),
                scales=plane[ROW[a] : P, lo:hi],
                in_=grouped[a][:, lo:hi, :].rearrange("p t j -> p (t j)"),
            )

        def gather_words(a, lo=0, hi=S):
            nc.vector.tensor_copy(slot_words[a][:, lo:hi], codes[a][:].bitcast(U32).indirect(offs_t[:, lo // 16 : hi // 16]))

        def gather_bytes(dst, plane):
            nc.vector.tensor_copy(dst[:], plane[:].indirect(offs_t[:]))

        banks = {}

        def multiply(a, experts):
            for e in experts:
                if a == ORDER[0]:
                    banks[e] = psum.tile([N, C], F32, name=f"bank{e % 8}")
                cols = slice(e * C, (e + 1) * C)
                if a < 2:
                    start = ((e % 4) * 2 + a) * 4 * N
                    lhsT, lscale = words[e // 4][:, start : start + 4 * N].bitcast(FP8X4), w8s[:, e, a, :]
                else:
                    start = 4 * 2 * 4 * N + ((e % 4) * 3 + a - 2) * 2 * N
                    lhsT, lscale = words[e // 4][:, start : start + 2 * N].bitcast(FP4X4), w4s[:, e, a - 2, :]
                if a == 2:
                    rscale = bytes_b[:, cols]
                elif a == 3:
                    rscale = moved[:, cols]
                else:
                    rscale = bytes_a[ROW[a] : P, cols]
                nc.tensor.matmul_mx(
                    out=banks[e][:], lhsT=lhsT, lhsT_scale=lscale,
                    rhs=slot_words[a][:, cols].bitcast(FP8X4), rhs_scale=rscale,
                    start=(a == ORDER[0]), stop=(a == ORDER[-1]),
                )

        def empty(e, on_vector=False):
            dst = y[:, e * C : (e + 1) * C]
            if on_vector:
                nc.vector.tensor_copy(dst, banks[e][:])
            else:
                nc.scalar.copy(dst, banks[e][:])

        cast(2, 0, 320, on_vector=True)
        cast(2, 320, 512)
        quantise(2, 0, 512)
        cast(2, 512, 640, on_vector=True)
        cast(2, 640, 768)
        quantise(2, 512, 768)
        for lo in (0, 256, 512):
            cast(3, lo, lo + 256)
        for a in (0, 1, 4):
            for lo, hi in PIECES:
                cast(a, lo, hi)
        gather_words(2)
        for lo, hi in PIECES:
            quantise(3, lo, hi)
        gather_words(3)
        gather_bytes(bytes_b, plane_b)
        for r in range(4):
            nc.sync.dma_start(moved[r:P:32, :].bitcast(I32), bytes_b[4 + r : P : 32, :].bitcast(I32))
        later = keep.tile([P, 2 * GROUP], U8, name="later", tag="shared", align_bytes=64)
        for g in (1, 2):
            words.append(later[:, (g - 1) * GROUP : g * GROUP])
            load_words(words[g], g)
        nc.sync.dma_start(pos1_t[:], pos1)
        nc.sync.dma_start(pos2_t[:], pos2)
        nc.sync.dma_start(gate_t[:], gate.rearrange("g p t -> p g t"))
        A, B, CD = range(0, 4), range(4, 8), range(8, 12)
        for experts in (A, B):
            for a in (2, 3):
                multiply(a, experts)
        for lo, hi in PIECES:
            quantise(0, lo, hi)
        gather_words(0, 0, 1024)
        for lo, hi in PIECES:
            quantise(1, lo, hi)
        gather_words(0, 1024, S)
        for lo, hi in PIECES:
            quantise(4, lo, hi)
        gather_bytes(bytes_a, plane_a)
        slot_words[1] = keep.tile([P, S], U32, name="slot_words1", tag="shared_a", align_bytes=64)
        multiply(0, A)
        multiply(0, B)
        for lo, experts in ((0, A), (512, B)):
            gather_words(1, lo, lo + 512)
            gather_words(4, lo, lo + 512)
            multiply(1, experts)
            multiply(4, experts)
            for e in experts:
                empty(e)
        gather_words(1, 1024, S)
        for a in (2, 3, 0, 1):
            multiply(a, CD)
        for lo in (1024, 1280):
            gather_words(4, lo, lo + 256)
            e = lo // C
            multiply(4, (e, e + 1))
            empty(e)
            empty(e + 1, on_vector=True)

        part = {}

        def finish(lo, hi):
            total = keep.tile([P, hi - lo], F32, name=f"total{lo}")
            nc.vector.tensor_tensor(total[:], part[lo, 0][:], part[lo, 1][:], ADD)
            nc.sync.dma_start(out[:, lo:hi], total[:])

        for lo, hi in ((0, 384), (384, 768)):
            for g, pos in enumerate((pos1_t, pos2_t)):
                part[lo, g] = keep.tile([P, hi - lo], F32, name=f"part{lo}_{g}")
                nc.vector.tensor_tensor(part[lo, g][:], y[:].indirect(pos[:, lo // 16 : hi // 16]), gate_t[:, g, lo:hi], MULT)
                if lo and g == 0:
                    finish(0, 384)
        finish(384, 768)
